import numpy as np
import ml_dtypes


def mxq(x, axis, fmt="e4m3"):
    dtype, down = {"e4m3": (ml_dtypes.float8_e4m3fn, 7), "e5m2": (ml_dtypes.float8_e5m2, 14)}[fmt]
    v = np.moveaxis(np.asarray(x, np.float32).astype(ml_dtypes.bfloat16).astype(np.float64), axis, -1)
    blocks = v.reshape(v.shape[:-1] + (-1, 32))
    amax = np.abs(blocks).max(-1, keepdims=True)
    byte = np.maximum(np.where(amax > 0, np.frexp(amax)[1] - 1 + 127, 0) - down, 1)
    scale = np.exp2(byte - 127.0)
    codes = (blocks / scale).astype(np.float32).astype(dtype).astype(np.float64)
    return np.moveaxis((codes * scale).reshape(v.shape), -1, axis)


WIDE = False


def mx_kscale(k):
    if not WIDE:
        return np.ones(k)
    levels = np.array([10, -10, 5, -5, 0])
    if k % 512:
        return np.exp2(np.random.permutation(np.resize(levels, k // 32))).repeat(32)
    a = np.empty((k // 512, 16))
    for p in range(k // 512):
        a[p, :8] = np.random.permutation(np.resize(levels, 8))
        for g in range(8):
            far = levels[np.abs(levels - a[p, g]) >= 10]
            a[p, g + 8] = far[np.random.randint(len(far))]
    return np.exp2(a.ravel()).repeat(32)


BF16 = ml_dtypes.bfloat16


def bf(x):
    return np.asarray(x, np.float32).astype(BF16)


def f64(x):
    return np.asarray(x).astype(np.float64)


E2M1 = np.array([0.0, 0.5, 1.0, 1.5, 2.0, 3.0, 4.0, 6.0, -0.0, -0.5, -1.0, -1.5, -2.0, -3.0, -4.0, -6.0])


def pack_weight(w, fmt):
    k, n = w.shape
    w = f64(bf(w)).reshape(k // 32, 32, n)
    amax = np.abs(w).max(1)
    if fmt == "e4m3":
        byte = np.frexp(amax)[1] - 1 + 127 - 7
    else:
        mant, ex = np.frexp(amax / 6.0)
        byte = np.where(mant > 0.5, ex, ex - 1) + 127
    byte = np.clip(np.where(amax > 0, byte, 1), 1, 254)
    scaled = (w * np.exp2(127.0 - byte)[:, None, :]).reshape(k, n).astype(np.float32)
    by_word = np.ascontiguousarray(scaled.reshape(k // 512, 128, 4, n).transpose(0, 1, 3, 2))
    if fmt == "e4m3":
        words = by_word.astype(ml_dtypes.float8_e4m3fn).view(np.uint8)
    else:
        c = by_word.astype(ml_dtypes.float4_e2m1fn).view(np.uint8) & 0xF
        words = c[..., 0::2] | (c[..., 1::2] << 4)
    return np.ascontiguousarray(words), np.ascontiguousarray(byte.astype(np.uint8).reshape(k // 512, 16, n))


def unpack_weight(words, scales, fmt):
    g, p, n, _ = words.shape
    if fmt == "e4m3":
        vals = np.ascontiguousarray(words).view(ml_dtypes.float8_e4m3fn).astype(np.float64)
    else:
        nib = np.empty((g, p, n, 4), np.uint8)
        nib[..., 0::2] = words & 0xF
        nib[..., 1::2] = words >> 4
        vals = E2M1[nib]
    vals = vals * np.repeat(np.exp2(scales.astype(np.float64) - 127.0), 8, axis=1)[..., None]
    return vals.transpose(0, 1, 3, 2).reshape(g * 512, n)
def pack4(w):
    words, scales = pack_weight(w, "e2m1")
    return words.reshape(words.shape[0], 128, -1), scales


def unpack4(words, scales):
    return unpack_weight(words.reshape(words.shape[0], 128, -1, 2), scales, "e2m1")


K, N = 2048, 1024


def setup_inputs():
    s, t = mx_kscale(K), mx_kscale(N)
    a = np.random.standard_normal((K, N)) * s[:, None]
    b = np.random.standard_normal((K, N)) / np.sqrt(K) / s[:, None]
    a_words, a_scales = pack4(a)
    b_words, b_scales = pack4(b)
    r = np.random.standard_normal((N, N))
    omega = (r - r.T) / np.sqrt(2 * N)
    gain = 1 + 0.1 * np.random.standard_normal(N)
    return {"a_words": a_words, "a_scales": a_scales,
            "b_words": b_words, "b_scales": b_scales,
            "d": bf(gain * t),
            "w": bf(omega / gain[:, None] / t[:, None])}


def reference(a_words, a_scales, b_words, b_scales, d, w):
    a = unpack4(a_words, a_scales)
    b = unpack4(b_words, b_scales)
    p = a.T @ b
    h = p + p.T
    hd = h * f64(d)
    c = mxq(hd, 1, "e4m3") @ mxq(f64(w), 0, "e4m3")
    return h + (c + c.T)

@@ -1,0 +1,372 @@
+from contextlib import ExitStack
+
+import concourse.mybir as mybir
+from concourse.masks import make_identity
+
+K, N = 2048, 1024
+FLOPS = 2 * K * N * N + 2 * N * N * N
+
+F32 = mybir.dt.float32
+BF16 = mybir.dt.bfloat16
+I32 = mybir.dt.int32
+U32 = mybir.dt.uint32
+U8 = mybir.dt.uint8
+FP4X4 = mybir.dt.float4_e2m1fn_x4
+FP8X4 = mybir.dt.float8_e4m3fn_x4
+ADD = mybir.AluOpType.add
+MULT = mybir.AluOpType.mult
+
+P = 128
+HALF = 512
+PACK = 4
+K_PASSES = K // HALF
+STORE_CUTS = {
+    (0, 0): ((0, 2), (2, 4)),
+    (0, 1): ((0, 2), (2, 4)),
+    (1, 0): ((0, 2), (2, 4)),
+    (1, 1): ((0, 1), (1, 3), (3, 4)),
+}
+DIAG_COLS = (((0, 512),), ((128, 256), (384, 128)), ((256, 256),), ((256, 256),))
+
+
+def tile_isospectral_bracket_step_s4_kernel(tc, a_words, a_scales, b_words, b_scales, d, w, out):
+    nc = tc.nc
+    words = (a_words, b_words)
+    scales = (a_scales, b_scales)
+
+    with ExitStack() as ctx:
+        keep = ctx.enter_context(tc.tile_pool(name="keep", bufs=1))
+        psum = ctx.enter_context(tc.psum_pool(name="psum", bufs=8))
+        ctx.enter_context(tc.manual_schedule())
+
+        def sb(name, shape, dtype):
+            return keep.tile(shape, dtype, name=name, align_bytes=64)
+
+        def bank():
+            return psum.tile([P, HALF], F32, name="bank")
+
+        raw_codes = [sb("raw_codes%d" % x, [P, K_PASSES, 2 * N], U8) for x in range(2)]
+        raw_scales = [sb("raw_scales%d" % x, [P, K_PASSES, N], U8) for x in range(2)]
+        codes = [[sb("codes%d%d" % (x, h), [P, K_PASSES, 2 * HALF], U8) for h in range(2)] for x in range(2)]
+        planes = [[sb("planes%d%d" % (x, h), [P, K_PASSES, HALF], U8) for h in range(2)] for x in range(2)]
+        w_raw = [sb("w_raw%d" % g, [P, PACK, N], BF16) for g in range(2)]
+        w_packed = [[sb("w_packed%d%d" % (g, h), [P, HALF, PACK], BF16) for h in range(2)] for g in range(2)]
+        w_codes = [[sb("w_codes%d%d" % (g, h), [P, HALF], U32) for h in range(2)] for g in range(2)]
+        w_planes = [[sb("w_planes%d%d" % (g, h), [P, HALF], U8) for h in range(2)] for g in range(2)]
+        hd_packed = [[sb("hd_packed%d%d" % (g, h), [P, HALF, PACK], BF16) for h in range(2)] for g in range(2)]
+        hd_codes = [[sb("hd_codes%d%d" % (g, h), [P, HALF], U32) for h in range(2)] for g in range(2)]
+        hd_planes = [[sb("hd_planes%d%d" % (g, h), [P, HALF], U8) for h in range(2)] for g in range(2)]
+        h_sb = {gh: sb("h_sb%d%d" % gh, [P, PACK, HALF], F32) for gh in ((0, 0), (0, 1), (1, 1))}
+        o_sb = {
+            (i, h, t0): sb("o_sb%d%d%d" % (i, h, t0), [P, t1 - t0, HALF], F32)
+            for (i, h), cuts in STORE_CUTS.items()
+            for t0, t1 in cuts
+        }
+
+        def o_rows(i, h, t):
+            t0 = max(c0 for c0, c1 in STORE_CUTS[i, h] if c0 <= t)
+            return o_sb[i, h, t0][:, t - t0, :]
+
+        d_runs = sb("d_runs", [P, 2, 16], BF16)
+        d_cols = sb("d_cols", [P, 2, PACK], F32)
+        ident = sb("ident", [P, P], F32)
+
+        def load_words(x, g0, g1):
+            nc.sync.dma_start(
+                out=raw_codes[x][:, g0:g1, :].bitcast(I32),
+                in_=words[x][g0:g1].bitcast(I32).rearrange("g p n -> p g n"),
+            )
+
+        def load_scales(queue, x, r, g0, g1):
+            queue.dma_start(
+                out=raw_scales[x][r:P:32, g0:g1, :].bitcast(I32),
+                in_=scales[x].bitcast(I32).rearrange("g (q r) n -> r q g n", r=4)[r][:, g0:g1, :],
+            )
+
+        def load_w(g, r):
+            rows = w[g * HALF : (g + 1) * HALF, :].rearrange("(m t r) n -> r m t n", t=4, r=4)
+            nc.sync.dma_start(out=w_raw[g][r:P:4, :, :], in_=rows[r])
+
+        def load_d(r):
+            runs = d.rearrange("(g m x) -> m g x", g=2, x=16)
+            nc.sync.dma_start(out=d_runs[r:P:4, :, 0:13], in_=runs[:, :, r : r + 13])
+
+        def reorder(x, g, h):
+            nc.vector.tensor_copy(
+                out=planes[x][h][:, g, :].bitcast(I32).rearrange("p (t m) -> p t m", t=4),
+                in_=raw_scales[x][:, g, h * HALF : (h + 1) * HALF].bitcast(I32).rearrange("p (m t) -> p t m", t=4),
+            )
+            nc.vector.tensor_copy(
+                out=codes[x][h][:, g, :].bitcast(I32).rearrange("p (t m e) -> p t m e", t=4, e=2),
+                in_=raw_codes[x][:, g, h * N : (h + 1) * N].bitcast(I32).rearrange("p (m t e) -> p t m e", t=4, e=2),
+            )
+
+        def ordered(x, g, h, c0, n):
+            return codes[x][h][:, g, 2 * c0 : 2 * (c0 + n)].bitcast(FP4X4), planes[x][h][:, g, c0 : c0 + n]
+
+        def natural(x, g, h):
+            return (
+                raw_codes[x][:, g, h * N : (h + 1) * N].bitcast(FP4X4),
+                raw_scales[x][:, g, h * HALF : (h + 1) * HALF],
+            )
+
+        def mx(acc, stationary, moving, start, stop):
+            nc.tensor.matmul_mx(
+                out=acc,
+                lhsT=stationary[0],
+                lhsT_scale=stationary[1],
+                rhs=moving[0],
+                rhs_scale=moving[1],
+                start=start,
+                stop=stop,
+            )
+
+        def off_diag_pass(acc, t, g, x):
+            mx(acc[:], ordered(x, g, 0, t * P, P), natural(1 - x, g, 1), g == 0 and x == 0, g == K_PASSES - 1 and x == 1)
+
+        def diag_pass(acc, h, t, c0, n, g, x):
+            mx(
+                acc[:, c0 : c0 + n],
+                ordered(x, g, h, t * P, P),
+                ordered(1 - x, g, h, c0, n),
+                g == 0 and x == 0,
+                g == K_PASSES - 1 and x == 1,
+            )
+
+        def diag_rows(h, t):
+            acc = bank()
+            for c0, n in DIAG_COLS[t]:
+                for g in range(K_PASSES):
+                    for x in range(2):
+                        diag_pass(acc, h, t, c0, n, g, x)
+            return acc
+
+        def keep_diag(acc, h, t):
+            c0 = DIAG_COLS[t][0][0]
+            nc.scalar.copy(out=h_sb[h, h][:, t, c0:], in_=acc[:, c0:])
+
+        def keep_off_diag(acc, t):
+            nc.scalar.copy(
+                out=h_sb[0, 1][:, t, :].rearrange("p (u m r) -> p u m r", u=4, r=4),
+                in_=acc[:].rearrange("p (m u r) -> p u m r", u=4, r=4),
+            )
+
+        def turn(src, cols):
+            acc = bank()
+            for i, c in enumerate(cols):
+                nc.tensor.transpose(acc[:, i * P : (i + 1) * P], src[:, c * P : (c + 1) * P], ident[:])
+            return acc
+
+        def mirror_turn(h):
+            return [turn(h_sb[h, h][:, t, :], range(t + 1, PACK)) for t in range(2)]
+
+        def mirror_keep(accs, h):
+            for t, acc in enumerate(accs):
+                n = PACK - 1 - t
+                nc.scalar.copy(
+                    out=h_sb[h, h][:, t + 1 :, t * P : (t + 1) * P],
+                    in_=acc[:, : n * P].rearrange("p (u c) -> p u c", u=n),
+                )
+
+        def pack_hd(g, h, c0, n):
+            nc.vector.tensor_tensor(
+                out=hd_packed[g][h][:, c0 : c0 + n, :].rearrange("p (c e) t -> p c t e", e=2),
+                in0=h_sb[g, h][:, :, c0 : c0 + n].rearrange("p t (c e) -> p c t e", e=2),
+                in1=d_cols[:, g, :].unsqueeze(1).unsqueeze(3).to_broadcast([P, n // 2, PACK, 2]),
+                op=MULT,
+            )
+
+        def pack_hd_turned(acc, t):
+            nc.vector.tensor_tensor(
+                out=hd_packed[1][0][:, t * P : (t + 1) * P, :],
+                in0=acc[:].rearrange("p (u c) -> p c u", u=4),
+                in1=d_cols[:, 1, :].unsqueeze(1).to_broadcast([P, P, PACK]),
+                op=MULT,
+            )
+
+        def pack_w(copy, g, h, u):
+            cols = w_raw[g][:, :, h * HALF : (h + 1) * HALF].rearrange("p t (m u r) -> p u m t r", u=4, r=4)
+            copy(
+                out=w_packed[g][h][:, u * P : (u + 1) * P, :].rearrange("p (m r) t -> p m t r", r=4),
+                in_=cols[:, u],
+            )
+
+        def quantize(dst_codes, dst_plane, src):
+            nc.vector.quantize_mx(
+                out=dst_codes[:].bitcast(FP8X4),
+                scales=dst_plane[:],
+                in_=src[:].rearrange("p c t -> p (c t)"),
+            )
+
+        def quantize_w(g, h):
+            quantize(w_codes[g][h], w_planes[g][h], w_packed[g][h])
+
+        def quantize_hd(g, h):
+            quantize(hd_codes[g][h], hd_planes[g][h], hd_packed[g][h])
+
+        def bracket_rows(i, t, h):
+            acc = bank()
+            cols = slice(t * P, (t + 1) * P)
+            for g in range(2):
+                mx(
+                    acc[:],
+                    (hd_codes[g][i][:, cols].bitcast(FP8X4), hd_planes[g][i][:, cols]),
+                    (w_codes[g][h][:].bitcast(FP8X4), w_planes[g][h][:]),
+                    g == 0,
+                    False,
+                )
+            for g in range(2):
+                mx(
+                    acc[:],
+                    (w_codes[g][i][:, cols].bitcast(FP8X4), w_planes[g][i][:, cols]),
+                    (hd_codes[g][h][:].bitcast(FP8X4), hd_planes[g][h][:]),
+                    False,
+                    g == 1,
+                )
+            return acc
+
+        def add_h(acc, i, t, h):
+            nc.vector.tensor_tensor(
+                out=o_rows(i, h, t).rearrange("p (m u r) -> p m u r", u=4, r=4),
+                in0=acc[:].rearrange("p (u m r) -> p m u r", u=4, r=4),
+                in1=h_sb[i, h][:, t, :].rearrange("p (u m r) -> p m u r", u=4, r=4),
+                op=ADD,
+            )
+
+        def store_rows(i, h, t0, t1):
+            rows = out[i * HALF : (i + 1) * HALF, h * HALF : (h + 1) * HALF].rearrange("(m t r) n -> r m t n", t=4, r=4)
+            for r in range(4):
+                nc.sync.dma_start(out=rows[r][:, t0:t1, :], in_=o_sb[i, h, t0][r:P:4, :, :])
+
+        nc.vector.memset(raw_scales[1][:].bitcast(I32), 0)
+        nc.vector.memset(raw_scales[0][:, 0, :].bitcast(I32), 0)
+        nc.vector.memset(raw_scales[0][:, 1:, :].bitcast(I32), 0)
+        for x in range(2):
+            load_words(x, 0, 1)
+        for r in range(2):
+            load_scales(nc.sync, 1, r, 0, 1)
+        for r in range(2, 4):
+            load_scales(nc.gpsimd, 1, r, 0, K_PASSES)
+        for r in range(4):
+            load_scales(nc.sync, 0, r, 0, 1)
+        for x in range(2):
+            load_words(x, 1, 2)
+        for r in range(4):
+            load_scales(nc.sync, 0, r, 1, K_PASSES)
+        for r in range(2):
+            load_scales(nc.sync, 1, r, 1, K_PASSES)
+        for x in range(2):
+            load_words(x, 2, K_PASSES)
+        for r in range(4):
+            load_w(0, r)
+        for r in range(4):
+            load_d(r)
+        for r in range(4):
+            load_w(1, r)
+        make_identity(nc, ident[:])
+
+        for g in range(K_PASSES):
+            for x in range(2):
+                reorder(x, g, 0)
+        for g in range(K_PASSES):
+            for x in range(2):
+                reorder(x, g, 1)
+
+        upper = [bank() for t in range(PACK)]
+        first = bank()
+        for g in range(2):
+            for x in range(2):
+                for t in range(PACK):
+                    off_diag_pass(upper[t], t, g, x)
+            for x in range(2):
+                diag_pass(first, 0, 0, 0, HALF, g, x)
+
+        for h in range(2):
+            for u in range(PACK):
+                pack_w(nc.vector.tensor_copy, 0, h, u)
+        nc.vector.tensor_copy(out=d_cols[:], in_=d_runs[:, :, 0:13:4])
+        for h in range(2):
+            quantize_w(0, h)
+
+        for t in range(PACK):
+            for g in range(2, K_PASSES):
+                for x in range(2):
+                    off_diag_pass(upper[t], t, g, x)
+            keep_off_diag(upper[t], t)
+        for g in range(2, K_PASSES):
+            for x in range(2):
+                diag_pass(first, 0, 0, 0, HALF, g, x)
+        pack_w(nc.scalar.copy, 1, 0, 0)
+        keep_diag(first, 0, 0)
+        for c in range(2):
+            pack_hd(0, 1, c * 2 * P, 2 * P)
+        acc = diag_rows(0, 1)
+        pack_w(nc.scalar.copy, 1, 0, 1)
+        pack_w(nc.scalar.copy, 1, 0, 2)
+        keep_diag(acc, 0, 1)
+
+        turned = [turn(h_sb[0, 1][:, t, :], range(PACK)) for t in range(PACK)]
+        mirrored = mirror_turn(0)
+        pack_w(nc.scalar.copy, 1, 0, 3)
+        for t in range(PACK):
+            pack_hd_turned(turned[t], t)
+        quantize_hd(0, 1)
+        mirror_keep(mirrored, 0)
+        quantize_w(1, 0)
+        quantize_hd(1, 0)
+        pack_hd(0, 0, 0, 2 * P)
+        for t in range(2, PACK):
+            acc = diag_rows(0, t)
+            keep_diag(acc, 0, t)
+            pack_w(nc.scalar.copy, 1, 1, t - 2)
+        pack_hd(0, 0, 2 * P, 2 * P)
+
+        for t in range(2):
+            acc = diag_rows(1, t)
+            pack_w(nc.scalar.copy, 1, 1, t + 2)
+            keep_diag(acc, 1, t)
+        quantize_hd(0, 0)
+        quantize_w(1, 1)
+        acc = diag_rows(1, 2)
+        mirrored = mirror_turn(1)
+        keep_diag(acc, 1, 2)
+        mirror_keep(mirrored, 1)
+        acc = diag_rows(1, 3)
+        keep_diag(acc, 1, 3)
+        pack_hd(1, 1, 0, 2 * P)
+
+        for t in range(PACK):
+            acc = bracket_rows(0, t, 0)
+            add_h(acc, 0, t, 0)
+            if t == 0:
+                pack_hd(1, 1, 2 * P, 2 * P)
+            if t == 1:
+                quantize_hd(1, 1)
+            if t % 2 == 1:
+                store_rows(0, 0, t - 1, t + 1)
+        for t in range(PACK):
+            acc = bracket_rows(0, t, 1)
+            add_h(acc, 0, t, 1)
+            if t % 2 == 1:
+                store_rows(0, 1, t - 1, t + 1)
+        acc = bracket_rows(1, 0, 1)
+        add_h(acc, 1, 0, 1)
+        store_rows(1, 1, 0, 1)
+
+        lower = out[HALF:, :HALF].rearrange("(s p) n -> p s n", p=P)
+        for s in range(PACK):
+            acc = bank()
+            for t in range(PACK):
+                nc.tensor.transpose(acc[:, t * P : (t + 1) * P], o_rows(0, 1, t)[:, s * P : (s + 1) * P], ident[:])
+            nc.scalar.copy(
+                out=o_rows(1, 0, s).rearrange("p (m t r) -> p m t r", t=4, r=4),
+                in_=acc[:].rearrange("p (t m r) -> p m t r", t=4, r=4),
+            )
+            if s % 2 == 1:
+                nc.sync.dma_start(out=lower[:, s - 1 : s + 1, :], in_=o_sb[1, 0, s - 1][:])
+        for t in range(1, PACK):
+            acc = bracket_rows(1, t, 1)
+            add_h(acc, 1, t, 1)
+            if t == 2:
+                store_rows(1, 1, 1, 3)
+        store_rows(1, 1, 3, 4)

@@ -21,12 +21,14 @@ HALF = 512
 PACK = 4
 K_PASSES = K // HALF
 STORE_CUTS = {
-    (0, 0): ((0, 2), (2, 4)),
+    (0, 0): ((0, 1), (1, 4)),
     (0, 1): ((0, 2), (2, 4)),
     (1, 0): ((0, 2), (2, 4)),
     (1, 1): ((0, 1), (1, 3), (3, 4)),
 }
-DIAG_COLS = (((0, 512),), ((128, 256), (384, 128)), ((256, 256),), ((256, 256),))
+DIAG_COLS = (((0, 512),), ((128, 256), (384, 128)), ((256, 256),), ((384, 128),))
+MIRROR = (((0, 1), (0, 2), (0, 3)), ((1, 2), (1, 3), (2, 3)))
+WARM_PASSES = 18
 
 
 def tile_isospectral_bracket_step_s4_kernel(tc, a_words, a_scales, b_words, b_scales, d, w, out):
@@ -45,8 +47,20 @@ def tile_isospectral_bracket_step_s4_kernel(tc, a_words, a_scales, b_words, b_sc
         def bank():
             return psum.tile([P, HALF], F32, name="bank")
 
-        raw_codes = [sb("raw_codes%d" % x, [P, K_PASSES, 2 * N], U8) for x in range(2)]
-        raw_scales = [sb("raw_scales%d" % x, [P, K_PASSES, N], U8) for x in range(2)]
+        code_loads = {
+            (x, g0): sb("raw_codes%d%d" % (x, g0), [P, g1 - g0, 2 * N], U8)
+            for x in range(2)
+            for g0, g1 in ((0, 1), (1, 2), (2, 4))
+        }
+        first_scales = [sb("first_scales%d" % x, [P, N], U8) for x in range(2)]
+        later_scales = [sb("later_scales%d" % x, [P, K_PASSES - 1, N], U8) for x in range(2)]
+
+        def raw_codes(x, g):
+            return code_loads[x, min(g, 2)][:, g - min(g, 2), :]
+
+        def raw_scales(x, g):
+            return first_scales[x][:] if g == 0 else later_scales[x][:, g - 1, :]
+
         codes = [[sb("codes%d%d" % (x, h), [P, K_PASSES, 2 * HALF], U8) for h in range(2)] for x in range(2)]
         planes = [[sb("planes%d%d" % (x, h), [P, K_PASSES, HALF], U8) for h in range(2)] for x in range(2)]
         w_raw = [sb("w_raw%d" % g, [P, PACK, N], BF16) for g in range(2)]
@@ -69,18 +83,26 @@ def tile_isospectral_bracket_step_s4_kernel(tc, a_words, a_scales, b_words, b_sc
 
         d_runs = sb("d_runs", [P, 2, 16], BF16)
         d_cols = sb("d_cols", [P, 2, PACK], F32)
+        s_upper = sb("s_upper", [P, PACK - 1, HALF], F32)
+        warm_in = sb("warm_in", [P, PACK * P], BF16)
+        warm_codes = sb("warm_codes", [P, P], U32)
+        warm_plane = sb("warm_plane", [P, P], U8)
         ident = sb("ident", [P, P], F32)
 
         def load_words(x, g0, g1):
             nc.sync.dma_start(
-                out=raw_codes[x][:, g0:g1, :].bitcast(I32),
+                out=code_loads[x, g0][:].bitcast(I32),
                 in_=words[x][g0:g1].bitcast(I32).rearrange("g p n -> p g n"),
             )
 
-        def load_scales(queue, x, r, g0, g1):
+        def load_first_scales(queue, x, q):
+            rows = scales[x].bitcast(I32).rearrange("g q n -> (g q) n")
+            queue.dma_start(out=first_scales[x][32 * q : 32 * (q + 1), :].bitcast(I32), in_=rows[4 * q : 4 * q + 32, :])
+
+        def load_later_scales(queue, x, r):
             queue.dma_start(
-                out=raw_scales[x][r:P:32, g0:g1, :].bitcast(I32),
-                in_=scales[x].bitcast(I32).rearrange("g (q r) n -> r q g n", r=4)[r][:, g0:g1, :],
+                out=later_scales[x][r:P:32, :, :].bitcast(I32),
+                in_=scales[x].bitcast(I32).rearrange("g (q r) n -> r q g n", r=4)[r][:, 1:, :],
             )
 
         def load_w(g, r):
@@ -94,11 +116,11 @@ def tile_isospectral_bracket_step_s4_kernel(tc, a_words, a_scales, b_words, b_sc
         def reorder(x, g, h):
             nc.vector.tensor_copy(
                 out=planes[x][h][:, g, :].bitcast(I32).rearrange("p (t m) -> p t m", t=4),
-                in_=raw_scales[x][:, g, h * HALF : (h + 1) * HALF].bitcast(I32).rearrange("p (m t) -> p t m", t=4),
+                in_=raw_scales(x, g)[:, h * HALF : (h + 1) * HALF].bitcast(I32).rearrange("p (m t) -> p t m", t=4),
             )
             nc.vector.tensor_copy(
                 out=codes[x][h][:, g, :].bitcast(I32).rearrange("p (t m e) -> p t m e", t=4, e=2),
-                in_=raw_codes[x][:, g, h * N : (h + 1) * N].bitcast(I32).rearrange("p (m t e) -> p t m e", t=4, e=2),
+                in_=raw_codes(x, g)[:, h * N : (h + 1) * N].bitcast(I32).rearrange("p (m t e) -> p t m e", t=4, e=2),
             )
 
         def ordered(x, g, h, c0, n):
@@ -106,8 +128,8 @@ def tile_isospectral_bracket_step_s4_kernel(tc, a_words, a_scales, b_words, b_sc
 
         def natural(x, g, h):
             return (
-                raw_codes[x][:, g, h * N : (h + 1) * N].bitcast(FP4X4),
-                raw_scales[x][:, g, h * HALF : (h + 1) * HALF],
+                raw_codes(x, g)[:, h * N : (h + 1) * N].bitcast(FP4X4),
+                raw_scales(x, g)[:, h * HALF : (h + 1) * HALF],
             )
 
         def mx(acc, stationary, moving, start, stop):
@@ -151,22 +173,24 @@ def tile_isospectral_bracket_step_s4_kernel(tc, a_words, a_scales, b_words, b_sc
                 in_=acc[:].rearrange("p (m u r) -> p u m r", u=4, r=4),
             )
 
-        def turn(src, cols):
+        def turn(blocks):
             acc = bank()
-            for i, c in enumerate(cols):
-                nc.tensor.transpose(acc[:, i * P : (i + 1) * P], src[:, c * P : (c + 1) * P], ident[:])
+            for i, block in enumerate(blocks):
+                nc.tensor.transpose(acc[:, i * P : (i + 1) * P], block, ident[:])
             return acc
 
-        def mirror_turn(h):
-            return [turn(h_sb[h, h][:, t, :], range(t + 1, PACK)) for t in range(2)]
+        def mirror_turn(src):
+            return [turn([src[:, t, u * P : (u + 1) * P] for t, u in pairs]) for pairs in MIRROR]
+
+        def mirror_parts(accs):
+            return [
+                (t, acc[:, c0 * P : (c0 + PACK - 1 - t) * P].rearrange("p (u c) -> p u c", c=P))
+                for t, acc, c0 in ((0, accs[0], 0), (1, accs[1], 0), (2, accs[1], 2))
+            ]
 
         def mirror_keep(accs, h):
-            for t, acc in enumerate(accs):
-                n = PACK - 1 - t
-                nc.scalar.copy(
-                    out=h_sb[h, h][:, t + 1 :, t * P : (t + 1) * P],
-                    in_=acc[:, : n * P].rearrange("p (u c) -> p u c", u=n),
-                )
+            for t, part in mirror_parts(accs):
+                nc.scalar.copy(out=h_sb[h, h][:, t + 1 :, t * P : (t + 1) * P], in_=part)
 
         def pack_hd(g, h, c0, n):
             nc.vector.tensor_tensor(
@@ -204,32 +228,31 @@ def tile_isospectral_bracket_step_s4_kernel(tc, a_words, a_scales, b_words, b_sc
         def quantize_hd(g, h):
             quantize(hd_codes[g][h], hd_planes[g][h], hd_packed[g][h])
 
-        def bracket_rows(i, t, h):
+        def bracket_pass(acc, i, t, h, c0, n, j):
+            g = j % 2
+            sides = ((hd_codes, hd_planes), (w_codes, w_planes))
+            (s_codes, s_planes), (m_codes, m_planes) = sides[j // 2], sides[1 - j // 2]
+            rows, cols = slice(t * P, (t + 1) * P), slice(c0, c0 + n)
+            mx(
+                acc[:, cols],
+                (s_codes[g][i][:, rows].bitcast(FP8X4), s_planes[g][i][:, rows]),
+                (m_codes[g][h][:, cols].bitcast(FP8X4), m_planes[g][h][:, cols]),
+                j == 0,
+                j == 3,
+            )
+
+        def bracket_rows(i, t, h, ranges):
             acc = bank()
-            cols = slice(t * P, (t + 1) * P)
-            for g in range(2):
-                mx(
-                    acc[:],
-                    (hd_codes[g][i][:, cols].bitcast(FP8X4), hd_planes[g][i][:, cols]),
-                    (w_codes[g][h][:].bitcast(FP8X4), w_planes[g][h][:]),
-                    g == 0,
-                    False,
-                )
-            for g in range(2):
-                mx(
-                    acc[:],
-                    (w_codes[g][i][:, cols].bitcast(FP8X4), w_planes[g][i][:, cols]),
-                    (hd_codes[g][h][:].bitcast(FP8X4), hd_planes[g][h][:]),
-                    False,
-                    g == 1,
-                )
+            for c0, n in ranges:
+                for j in range(4):
+                    bracket_pass(acc, i, t, h, c0, n, j)
             return acc
 
-        def add_h(acc, i, t, h):
+        def add_h(acc, i, t, h, u0):
             nc.vector.tensor_tensor(
-                out=o_rows(i, h, t).rearrange("p (m u r) -> p m u r", u=4, r=4),
-                in0=acc[:].rearrange("p (u m r) -> p m u r", u=4, r=4),
-                in1=h_sb[i, h][:, t, :].rearrange("p (u m r) -> p m u r", u=4, r=4),
+                out=o_rows(i, h, t).rearrange("p (m u r) -> p m u r", u=4, r=4)[:, :, u0:, :],
+                in0=acc[:].rearrange("p (u m r) -> p m u r", u=4, r=4)[:, :, u0:, :],
+                in1=h_sb[i, h][:, t, :].rearrange("p (u m r) -> p m u r", u=4, r=4)[:, :, u0:, :],
                 op=ADD,
             )
 
@@ -238,23 +261,24 @@ def tile_isospectral_bracket_step_s4_kernel(tc, a_words, a_scales, b_words, b_sc
             for r in range(4):
                 nc.sync.dma_start(out=rows[r][:, t0:t1, :], in_=o_sb[i, h, t0][r:P:4, :, :])
 
-        nc.vector.memset(raw_scales[1][:].bitcast(I32), 0)
-        nc.vector.memset(raw_scales[0][:, 0, :].bitcast(I32), 0)
-        nc.vector.memset(raw_scales[0][:, 1:, :].bitcast(I32), 0)
+        for q in range(2):
+            load_first_scales(nc.sync, 1, q)
         for x in range(2):
             load_words(x, 0, 1)
-        for r in range(2):
-            load_scales(nc.sync, 1, r, 0, 1)
-        for r in range(2, 4):
-            load_scales(nc.gpsimd, 1, r, 0, K_PASSES)
-        for r in range(4):
-            load_scales(nc.sync, 0, r, 0, 1)
+        for q in range(4):
+            load_first_scales(nc.sync, 0, q)
+        for q in range(2, 4):
+            load_first_scales(nc.sync, 1, q)
+        nc.vector.memset(warm_in[:], 1.0)
+        nc.vector.quantize_mx(out=warm_codes[:].bitcast(FP8X4), scales=warm_plane[:], in_=warm_in[:])
+        nc.vector.memset(later_scales[1][:].bitcast(I32), 0)
+        nc.vector.memset(later_scales[0][:].bitcast(I32), 0)
         for x in range(2):
             load_words(x, 1, 2)
         for r in range(4):
-            load_scales(nc.sync, 0, r, 1, K_PASSES)
-        for r in range(2):
-            load_scales(nc.sync, 1, r, 1, K_PASSES)
+            load_later_scales(nc.sync, 0, r)
+        for r in range(4):
+            load_later_scales(nc.sync if r < 2 else nc.gpsimd, 1, r)
         for x in range(2):
             load_words(x, 2, K_PASSES)
         for r in range(4):
@@ -265,22 +289,15 @@ def tile_isospectral_bracket_step_s4_kernel(tc, a_words, a_scales, b_words, b_sc
             load_w(1, r)
         make_identity(nc, ident[:])
 
-        for g in range(K_PASSES):
-            for x in range(2):
-                reorder(x, g, 0)
-        for g in range(K_PASSES):
-            for x in range(2):
-                reorder(x, g, 1)
+        acc = bank()
+        warm = (warm_codes[:].bitcast(FP8X4), warm_plane[:])
+        for i in range(WARM_PASSES):
+            mx(acc[:, :P], warm, warm, True, True)
 
-        upper = [bank() for t in range(PACK)]
-        first = bank()
-        for g in range(2):
-            for x in range(2):
-                for t in range(PACK):
-                    off_diag_pass(upper[t], t, g, x)
-            for x in range(2):
-                diag_pass(first, 0, 0, 0, HALF, g, x)
-
+        for h in range(2):
+            for g in range(K_PASSES):
+                for x in range(2):
+                    reorder(x, g, h)
         for h in range(2):
             for u in range(PACK):
                 pack_w(nc.vector.tensor_copy, 0, h, u)
@@ -288,85 +305,104 @@ def tile_isospectral_bracket_step_s4_kernel(tc, a_words, a_scales, b_words, b_sc
         for h in range(2):
             quantize_w(0, h)
 
+        upper = [bank() for t in range(PACK)]
+        diag = [bank() for t in range(PACK)]
+        for x in range(2):
+            for t in range(PACK):
+                off_diag_pass(upper[t], t, 0, x)
+        for t in range(PACK):
+            for x in range(2):
+                diag_pass(diag[t], 0, t, *DIAG_COLS[t][0], 0, x)
+        for x in range(2):
+            for t in range(PACK):
+                off_diag_pass(upper[t], t, 1, x)
+        for t in range(PACK):
+            for i, (c0, n) in enumerate(DIAG_COLS[t]):
+                for g in range(1 if i == 0 else 0, K_PASSES):
+                    for x in range(2):
+                        diag_pass(diag[t], 0, t, c0, n, g, x)
+            keep_diag(diag[t], 0, t)
         for t in range(PACK):
             for g in range(2, K_PASSES):
                 for x in range(2):
                     off_diag_pass(upper[t], t, g, x)
             keep_off_diag(upper[t], t)
-        for g in range(2, K_PASSES):
-            for x in range(2):
-                diag_pass(first, 0, 0, 0, HALF, g, x)
-        pack_w(nc.scalar.copy, 1, 0, 0)
-        keep_diag(first, 0, 0)
+            if t == 0:
+                mirror_keep(mirror_turn(h_sb[0, 0]), 0)
+                for c in range(2):
+                    pack_hd(0, 0, c * 2 * P, 2 * P)
+                quantize_hd(0, 0)
+            else:
+                pack_w(nc.scalar.copy, 1, 0, t - 1)
         for c in range(2):
             pack_hd(0, 1, c * 2 * P, 2 * P)
-        acc = diag_rows(0, 1)
-        pack_w(nc.scalar.copy, 1, 0, 1)
-        pack_w(nc.scalar.copy, 1, 0, 2)
-        keep_diag(acc, 0, 1)
 
-        turned = [turn(h_sb[0, 1][:, t, :], range(PACK)) for t in range(PACK)]
-        mirrored = mirror_turn(0)
+        acc = diag_rows(1, 0)
         pack_w(nc.scalar.copy, 1, 0, 3)
+        pack_w(nc.scalar.copy, 1, 1, 0)
+        keep_diag(acc, 1, 0)
+        turned = [turn([h_sb[0, 1][:, t, u * P : (u + 1) * P] for u in range(PACK)]) for t in range(PACK)]
         for t in range(PACK):
             pack_hd_turned(turned[t], t)
-        quantize_hd(0, 1)
-        mirror_keep(mirrored, 0)
+        for u in range(1, PACK):
+            pack_w(nc.scalar.copy, 1, 1, u)
         quantize_w(1, 0)
+        quantize_hd(0, 1)
         quantize_hd(1, 0)
-        pack_hd(0, 0, 0, 2 * P)
-        for t in range(2, PACK):
-            acc = diag_rows(0, t)
-            keep_diag(acc, 0, t)
-            pack_w(nc.scalar.copy, 1, 1, t - 2)
-        pack_hd(0, 0, 2 * P, 2 * P)
-
-        for t in range(2):
-            acc = diag_rows(1, t)
-            pack_w(nc.scalar.copy, 1, 1, t + 2)
-            keep_diag(acc, 1, t)
-        quantize_hd(0, 0)
         quantize_w(1, 1)
-        acc = diag_rows(1, 2)
-        mirrored = mirror_turn(1)
-        keep_diag(acc, 1, 2)
-        mirror_keep(mirrored, 1)
-        acc = diag_rows(1, 3)
-        keep_diag(acc, 1, 3)
-        pack_hd(1, 1, 0, 2 * P)
+        for t in range(1, PACK):
+            keep_diag(diag_rows(1, t), 1, t)
+        pack_hd(1, 1, 3 * P, P)
+        mirror_keep(mirror_turn(h_sb[1, 1]), 1)
+        pack_hd(1, 1, 0, P)
+        pack_hd(1, 1, P, 2 * P)
 
-        for t in range(PACK):
-            acc = bracket_rows(0, t, 0)
-            add_h(acc, 0, t, 0)
+        for t in range(PACK - 1):
+            acc = bracket_rows(0, t, 0, DIAG_COLS[t])
+            nc.scalar.copy(out=s_upper[:, t, (t + 1) * P :], in_=acc[:, (t + 1) * P :])
+            add_h(acc, 0, t, 0, t)
             if t == 0:
-                pack_hd(1, 1, 2 * P, 2 * P)
-            if t == 1:
                 quantize_hd(1, 1)
-            if t % 2 == 1:
-                store_rows(0, 0, t - 1, t + 1)
-        for t in range(PACK):
-            acc = bracket_rows(0, t, 1)
-            add_h(acc, 0, t, 1)
-            if t % 2 == 1:
-                store_rows(0, 1, t - 1, t + 1)
-        acc = bracket_rows(1, 0, 1)
-        add_h(acc, 1, 0, 1)
-        store_rows(1, 1, 0, 1)
+                store_rows(0, 0, 0, 1)
+        pair = [bank() for t in range(2)]
+        for t in range(2):
+            for j in range(3):
+                bracket_pass(pair[t], 0, t, 1, 0, HALF, j)
+        for t in range(2):
+            bracket_pass(pair[t], 0, t, 1, 0, HALF, 3)
+            add_h(pair[t], 0, t, 1, 0)
+        store_rows(0, 1, 0, 2)
+        for t in range(2, PACK):
+            add_h(bracket_rows(0, t, 1, DIAG_COLS[0]), 0, t, 1, 0)
+        store_rows(0, 1, 2, 4)
+        add_h(bracket_rows(0, PACK - 1, 0, DIAG_COLS[PACK - 1]), 0, PACK - 1, 0, PACK - 1)
 
+        below = o_sb[0, 0, 1][:].rearrange("p c (m u r) -> p u c m r", u=4, r=4)
+        for t, part in mirror_parts(mirror_turn(s_upper)):
+            nc.vector.tensor_tensor(
+                out=below[:, t, t:],
+                in0=part.rearrange("p c (m r) -> p c m r", r=4),
+                in1=h_sb[0, 0][:, t + 1 :, t * P : (t + 1) * P].rearrange("p c (m r) -> p c m r", r=4),
+                op=ADD,
+            )
+        store_rows(0, 0, 1, 4)
+
+        flipped = [bank() for s in range(PACK)]
+        for t in range(PACK):
+            for s in range(PACK):
+                nc.tensor.transpose(flipped[s][:, t * P : (t + 1) * P], o_rows(0, 1, t)[:, s * P : (s + 1) * P], ident[:])
         lower = out[HALF:, :HALF].rearrange("(s p) n -> p s n", p=P)
         for s in range(PACK):
-            acc = bank()
-            for t in range(PACK):
-                nc.tensor.transpose(acc[:, t * P : (t + 1) * P], o_rows(0, 1, t)[:, s * P : (s + 1) * P], ident[:])
             nc.scalar.copy(
                 out=o_rows(1, 0, s).rearrange("p (m t r) -> p m t r", t=4, r=4),
-                in_=acc[:].rearrange("p (t m r) -> p m t r", t=4, r=4),
+                in_=flipped[s][:].rearrange("p (t m r) -> p m t r", t=4, r=4),
             )
-            if s % 2 == 1:
-                nc.sync.dma_start(out=lower[:, s - 1 : s + 1, :], in_=o_sb[1, 0, s - 1][:])
-        for t in range(1, PACK):
-            acc = bracket_rows(1, t, 1)
-            add_h(acc, 1, t, 1)
+        nc.sync.dma_start(out=lower[:, 0:2, :], in_=o_sb[1, 0, 0][:])
+        for t in range(PACK):
+            add_h(bracket_rows(1, t, 1, DIAG_COLS[0]), 1, t, 1, 0)
+            if t == 0:
+                store_rows(1, 1, 0, 1)
+                nc.sync.dma_start(out=lower[:, 2:4, :], in_=o_sb[1, 0, 2][:])
             if t == 2:
                 store_rows(1, 1, 1, 3)
         store_rows(1, 1, 3, 4)

@@ -27,6 +27,13 @@ STORE_CUTS = {
     (1, 1): ((0, 1), (1, 3), (3, 4)),
 }
 DIAG_COLS = (((0, 512),), ((128, 256), (384, 128)), ((256, 256),), ((384, 128),))
+H_GROUPS = (
+    (((0, 512), ((128, 128), (256, 256))),),
+    (((256, 256), ((256, 256),)), ((128, 128), ())),
+    (((256, 256), ((384, 128),)),),
+    (((384, 128), ()),),
+)
+ROW_GROUPS = ((0,), (1,), (2, 3))
 MIRROR = (((0, 1), (0, 2), (0, 3)), ((1, 2), (1, 3), (2, 3)))
 WARM_PASSES = 18
 
@@ -70,7 +77,7 @@ def tile_isospectral_bracket_step_s4_kernel(tc, a_words, a_scales, b_words, b_sc
         hd_packed = [[sb("hd_packed%d%d" % (g, h), [P, HALF, PACK], BF16) for h in range(2)] for g in range(2)]
         hd_codes = [[sb("hd_codes%d%d" % (g, h), [P, HALF], U32) for h in range(2)] for g in range(2)]
         hd_planes = [[sb("hd_planes%d%d" % (g, h), [P, HALF], U8) for h in range(2)] for g in range(2)]
-        h_sb = {gh: sb("h_sb%d%d" % gh, [P, PACK, HALF], F32) for gh in ((0, 0), (0, 1), (1, 1))}
+        h_sb = {gh: sb("h_sb%d%d" % gh, [P, PACK, PACK, P], F32) for gh in ((0, 0), (0, 1), (1, 1))}
         o_sb = {
             (i, h, t0): sb("o_sb%d%d%d" % (i, h, t0), [P, t1 - t0, HALF], F32)
             for (i, h), cuts in STORE_CUTS.items()
@@ -81,9 +88,10 @@ def tile_isospectral_bracket_step_s4_kernel(tc, a_words, a_scales, b_words, b_sc
             t0 = max(c0 for c0, c1 in STORE_CUTS[i, h] if c0 <= t)
             return o_sb[i, h, t0][:, t - t0, :]
 
+        hd_rows = [sb("hd_rows%d" % g, [P, PACK, HALF // (g + 1)], BF16) for g in range(2)]
         d_runs = sb("d_runs", [P, 2, 16], BF16)
         d_cols = sb("d_cols", [P, 2, PACK], F32)
-        s_upper = sb("s_upper", [P, PACK - 1, HALF], F32)
+        s_upper = [sb("s_upper%d" % h, [P, PACK - 1 - 2 * h, HALF], F32) for h in range(2)]
         warm_in = sb("warm_in", [P, PACK * P], BF16)
         warm_codes = sb("warm_codes", [P, P], U32)
         warm_plane = sb("warm_plane", [P, P], U8)
@@ -146,31 +154,54 @@ def tile_isospectral_bracket_step_s4_kernel(tc, a_words, a_scales, b_words, b_sc
         def off_diag_pass(acc, t, g, x):
             mx(acc[:], ordered(x, g, 0, t * P, P), natural(1 - x, g, 1), g == 0 and x == 0, g == K_PASSES - 1 and x == 1)
 
-        def diag_pass(acc, h, t, c0, n, g, x):
-            mx(
-                acc[:, c0 : c0 + n],
-                ordered(x, g, h, t * P, P),
-                ordered(1 - x, g, h, c0, n),
-                g == 0 and x == 0,
-                g == K_PASSES - 1 and x == 1,
-            )
+        def diag_passes(acc, h, t, group, g):
+            ab, ba = group
+            passes = [(0, ab)] + [(1, cols) for cols in ba]
+            for x, (c0, n) in passes[::-1] if g == K_PASSES - 1 else passes:
+                mx(
+                    acc[:, c0 : c0 + n],
+                    ordered(x, g, h, t * P, P),
+                    ordered(1 - x, g, h, c0, n),
+                    g == 0 and x == 0,
+                    g == K_PASSES - 1 and x == 0,
+                )
 
         def diag_rows(h, t):
             acc = bank()
-            for c0, n in DIAG_COLS[t]:
+            for group in H_GROUPS[t]:
                 for g in range(K_PASSES):
-                    for x in range(2):
-                        diag_pass(acc, h, t, c0, n, g, x)
+                    diag_passes(acc, h, t, group, g)
             return acc
 
         def keep_diag(acc, h, t):
-            c0 = DIAG_COLS[t][0][0]
-            nc.scalar.copy(out=h_sb[h, h][:, t, c0:], in_=acc[:, c0:])
+            nc.scalar.copy(out=h_sb[h, h][:, t:, t, :], in_=acc[:, t * P :].rearrange("p (u c) -> p u c", c=P))
 
         def keep_off_diag(acc, t):
             nc.scalar.copy(
-                out=h_sb[0, 1][:, t, :].rearrange("p (u m r) -> p u m r", u=4, r=4),
+                out=h_sb[0, 1][:, :, t, :].rearrange("p u (m r) -> p u m r", r=4),
                 in_=acc[:].rearrange("p (m u r) -> p u m r", u=4, r=4),
+            )
+
+        def scale_off_diag(acc, t):
+            nc.scalar.activation(
+                out=hd_rows[0][:, t, :].rearrange("p (u m r) -> p u m r", u=4, r=4),
+                in_=acc[:].rearrange("p (m u r) -> p u m r", u=4, r=4),
+                func=mybir.ActivationFunctionType.Copy,
+                scale=d_cols[:, 0, t : t + 1],
+            )
+
+        def scale_last_cols(t):
+            nc.scalar.activation(
+                out=hd_rows[1][:, t, :].rearrange("p (u c) -> p u c", c=P),
+                in_=h_sb[1, 1][:, 2:, t, :],
+                func=mybir.ActivationFunctionType.Copy,
+                scale=d_cols[:, 1, t : t + 1],
+            )
+
+        def pack_hd_rows(g, c0):
+            nc.vector.tensor_copy(
+                out=hd_packed[g][1][:, c0:, :].rearrange("p (c e) t -> p c t e", e=4),
+                in_=hd_rows[g][:].rearrange("p t (c e) -> p c t e", e=4),
             )
 
         def turn(blocks):
@@ -188,15 +219,25 @@ def tile_isospectral_bracket_step_s4_kernel(tc, a_words, a_scales, b_words, b_sc
                 for t, acc, c0 in ((0, accs[0], 0), (1, accs[1], 0), (2, accs[1], 2))
             ]
 
-        def mirror_keep(accs, h):
-            for t, part in mirror_parts(accs):
-                nc.scalar.copy(out=h_sb[h, h][:, t + 1 :, t * P : (t + 1) * P], in_=part)
+        def turn_rows(h, rows):
+            return turn([h_sb[h, h][:, u, t, :] for t in rows for u in range(t, PACK)])
 
-        def pack_hd(g, h, c0, n):
+        def complete_rows(acc, h, rows):
+            starts = [sum(PACK - t for t in rows[:i]) * P for i in range(len(rows))]
+            t = rows[0]
+            nc.scalar.copy(
+                out=h_sb[h, h][:, t, t + 1 :, :],
+                in_=acc[:, P : (PACK - t) * P].rearrange("p (u c) -> p u c", c=P),
+            )
+            for t, c0 in zip(rows, starts):
+                block = h_sb[h, h][:, t, t, :]
+                nc.vector.tensor_tensor(out=block, in0=acc[:, c0 : c0 + P], in1=block, op=ADD)
+
+        def pack_hd(g, h, u):
             nc.vector.tensor_tensor(
-                out=hd_packed[g][h][:, c0 : c0 + n, :].rearrange("p (c e) t -> p c t e", e=2),
-                in0=h_sb[g, h][:, :, c0 : c0 + n].rearrange("p t (c e) -> p c t e", e=2),
-                in1=d_cols[:, g, :].unsqueeze(1).unsqueeze(3).to_broadcast([P, n // 2, PACK, 2]),
+                out=hd_packed[g][h][:, u * P : (u + 1) * P, :].rearrange("p (c e) t -> p c t e", e=2),
+                in0=h_sb[g, h][:, u].rearrange("p t (c e) -> p c t e", e=2),
+                in1=d_cols[:, g, :].unsqueeze(1).unsqueeze(3).to_broadcast([P, P // 2, PACK, 2]),
                 op=MULT,
             )
 
@@ -252,7 +293,7 @@ def tile_isospectral_bracket_step_s4_kernel(tc, a_words, a_scales, b_words, b_sc
             nc.vector.tensor_tensor(
                 out=o_rows(i, h, t).rearrange("p (m u r) -> p m u r", u=4, r=4)[:, :, u0:, :],
                 in0=acc[:].rearrange("p (u m r) -> p m u r", u=4, r=4)[:, :, u0:, :],
-                in1=h_sb[i, h][:, t, :].rearrange("p (u m r) -> p m u r", u=4, r=4)[:, :, u0:, :],
+                in1=h_sb[i, h][:, u0:, t, :].rearrange("p u (m r) -> p m u r", r=4),
                 op=ADD,
             )
 
@@ -261,13 +302,18 @@ def tile_isospectral_bracket_step_s4_kernel(tc, a_words, a_scales, b_words, b_sc
             for r in range(4):
                 nc.sync.dma_start(out=rows[r][:, t0:t1, :], in_=o_sb[i, h, t0][r:P:4, :, :])
 
+        def store_done(i, h, t):
+            for t0, t1 in STORE_CUTS[i, h]:
+                if t1 == t + 1:
+                    store_rows(i, h, t0, t1)
+
         for q in range(2):
-            load_first_scales(nc.sync, 1, q)
-        for x in range(2):
-            load_words(x, 0, 1)
-        for q in range(4):
             load_first_scales(nc.sync, 0, q)
+        load_words(0, 0, 1)
         for q in range(2, 4):
+            load_first_scales(nc.sync, 0, q)
+        load_words(1, 0, 1)
+        for q in range(4):
             load_first_scales(nc.sync, 1, q)
         nc.vector.memset(warm_in[:], 1.0)
         nc.vector.quantize_mx(out=warm_codes[:].bitcast(FP8X4), scales=warm_plane[:], in_=warm_in[:])
@@ -294,115 +340,139 @@ def tile_isospectral_bracket_step_s4_kernel(tc, a_words, a_scales, b_words, b_sc
         for i in range(WARM_PASSES):
             mx(acc[:, :P], warm, warm, True, True)
 
-        for h in range(2):
-            for g in range(K_PASSES):
-                for x in range(2):
-                    reorder(x, g, h)
+        for g, h in ((0, 0), (0, 1), (1, 0), (1, 1), (2, 0), (3, 0), (2, 1), (3, 1)):
+            for x in range(2):
+                reorder(x, g, h)
+        nc.vector.tensor_copy(out=d_cols[:], in_=d_runs[:, :, 0:13:4])
         for h in range(2):
             for u in range(PACK):
                 pack_w(nc.vector.tensor_copy, 0, h, u)
-        nc.vector.tensor_copy(out=d_cols[:], in_=d_runs[:, :, 0:13:4])
-        for h in range(2):
-            quantize_w(0, h)
+        quantize_w(0, 0)
 
         upper = [bank() for t in range(PACK)]
         diag = [bank() for t in range(PACK)]
-        for x in range(2):
-            for t in range(PACK):
-                off_diag_pass(upper[t], t, 0, x)
-        for t in range(PACK):
+        for g in range(2):
             for x in range(2):
-                diag_pass(diag[t], 0, t, *DIAG_COLS[t][0], 0, x)
-        for x in range(2):
+                for t in range(PACK):
+                    off_diag_pass(upper[t], t, g, x)
             for t in range(PACK):
-                off_diag_pass(upper[t], t, 1, x)
+                diag_passes(diag[t], 0, t, H_GROUPS[t][0], g)
         for t in range(PACK):
-            for i, (c0, n) in enumerate(DIAG_COLS[t]):
-                for g in range(1 if i == 0 else 0, K_PASSES):
-                    for x in range(2):
-                        diag_pass(diag[t], 0, t, c0, n, g, x)
+            for i, group in enumerate(H_GROUPS[t]):
+                for g in range(2 if i == 0 else 0, K_PASSES):
+                    diag_passes(diag[t], 0, t, group, g)
             keep_diag(diag[t], 0, t)
-        for t in range(PACK):
+        for g in range(2, K_PASSES):
+            for x in range(2):
+                off_diag_pass(upper[0], 0, g, x)
+        keep_off_diag(upper[0], 0)
+        turned = [turn_rows(0, rows) for rows in ROW_GROUPS]
+        for acc, rows in zip(turned, ROW_GROUPS):
+            complete_rows(acc, 0, rows)
+        scale_off_diag(upper[0], 0)
+        for u in range(PACK):
+            pack_hd(0, 0, u)
+        quantize_w(0, 1)
+        quantize_hd(0, 0)
+        for t in range(1, PACK):
             for g in range(2, K_PASSES):
                 for x in range(2):
                     off_diag_pass(upper[t], t, g, x)
             keep_off_diag(upper[t], t)
-            if t == 0:
-                mirror_keep(mirror_turn(h_sb[0, 0]), 0)
-                for c in range(2):
-                    pack_hd(0, 0, c * 2 * P, 2 * P)
-                quantize_hd(0, 0)
-            else:
-                pack_w(nc.scalar.copy, 1, 0, t - 1)
-        for c in range(2):
-            pack_hd(0, 1, c * 2 * P, 2 * P)
+            if t < PACK - 1:
+                scale_off_diag(upper[t], t)
 
         acc = diag_rows(1, 0)
-        pack_w(nc.scalar.copy, 1, 0, 3)
-        pack_w(nc.scalar.copy, 1, 1, 0)
+        scale_off_diag(upper[PACK - 1], PACK - 1)
+        pack_w(nc.scalar.copy, 1, 0, 0)
         keep_diag(acc, 1, 0)
-        turned = [turn([h_sb[0, 1][:, t, u * P : (u + 1) * P] for u in range(PACK)]) for t in range(PACK)]
+        pack_hd_rows(0, 0)
+        turned = [turn([h_sb[0, 1][:, u, t, :] for u in range(PACK)]) for t in range(PACK)]
+        acc = turn_rows(1, ROW_GROUPS[0])
         for t in range(PACK):
             pack_hd_turned(turned[t], t)
-        for u in range(1, PACK):
-            pack_w(nc.scalar.copy, 1, 1, u)
-        quantize_w(1, 0)
+        for u in range(1, 3):
+            pack_w(nc.scalar.copy, 1, 0, u)
+        complete_rows(acc, 1, ROW_GROUPS[0])
+        pack_w(nc.scalar.copy, 1, 0, 3)
         quantize_hd(0, 1)
         quantize_hd(1, 0)
-        quantize_w(1, 1)
+        quantize_w(1, 0)
+        pack_w(nc.scalar.copy, 1, 1, 0)
+        pack_w(nc.vector.tensor_copy, 1, 1, 1)
+        pack_hd(1, 1, 0)
         for t in range(1, PACK):
             keep_diag(diag_rows(1, t), 1, t)
-        pack_hd(1, 1, 3 * P, P)
-        mirror_keep(mirror_turn(h_sb[1, 1]), 1)
-        pack_hd(1, 1, 0, P)
-        pack_hd(1, 1, P, 2 * P)
+        turned = [turn_rows(1, rows) for rows in ROW_GROUPS[1:]]
+        for acc, rows in zip(turned, ROW_GROUPS[1:]):
+            complete_rows(acc, 1, rows)
+        pack_hd(1, 1, 1)
 
-        for t in range(PACK - 1):
-            acc = bracket_rows(0, t, 0, DIAG_COLS[t])
-            nc.scalar.copy(out=s_upper[:, t, (t + 1) * P :], in_=acc[:, (t + 1) * P :])
-            add_h(acc, 0, t, 0, t)
-            if t == 0:
-                quantize_hd(1, 1)
-                store_rows(0, 0, 0, 1)
+        def add_mirrored(i, t, part, dst):
+            nc.vector.tensor_tensor(
+                out=dst.rearrange("p c (m u r) -> p u c m r", u=4, r=4)[:, t],
+                in0=part.rearrange("p c (m r) -> p c m r", r=4),
+                in1=h_sb[i, i][:, t, t + 1 :, :].rearrange("p c (m r) -> p c m r", r=4),
+                op=ADD,
+            )
+
+        accs = []
+        for t in range(PACK):
+            accs.append(bracket_rows(0, t, 0, DIAG_COLS[t]))
+            if t < PACK - 1:
+                if t < 2:
+                    pack_w(nc.scalar.copy, 1, 1, t + 2)
+                nc.scalar.copy(out=s_upper[0][:, t, (t + 1) * P :], in_=accs[t][:, (t + 1) * P :])
+        pack_hd(1, 1, 2)
+        pack_hd(1, 1, 3)
+        add_h(accs[0], 0, 0, 0, 0)
+        store_rows(0, 0, 0, 1)
+        quantize_w(1, 1)
+        quantize_hd(1, 1)
+        add_h(accs[1], 0, 1, 0, 1)
+        add_h(accs[2], 0, 2, 0, 2)
+        add_h(accs[3], 0, 3, 0, 3)
         pair = [bank() for t in range(2)]
         for t in range(2):
-            for j in range(3):
+            for j in (0, 2):
                 bracket_pass(pair[t], 0, t, 1, 0, HALF, j)
+        for t, part in mirror_parts(mirror_turn(s_upper[0])):
+            add_mirrored(0, t, part, o_sb[0, 0, 1][:, t:, :])
+        store_rows(0, 0, 1, 4)
+        for t in range(2):
+            bracket_pass(pair[t], 0, t, 1, 0, HALF, 1)
         for t in range(2):
             bracket_pass(pair[t], 0, t, 1, 0, HALF, 3)
             add_h(pair[t], 0, t, 1, 0)
-        store_rows(0, 1, 0, 2)
+        store_done(0, 1, 1)
         for t in range(2, PACK):
             add_h(bracket_rows(0, t, 1, DIAG_COLS[0]), 0, t, 1, 0)
-        store_rows(0, 1, 2, 4)
-        add_h(bracket_rows(0, PACK - 1, 0, DIAG_COLS[PACK - 1]), 0, PACK - 1, 0, PACK - 1)
+            store_done(0, 1, t)
+        acc = bracket_rows(1, 0, 1, DIAG_COLS[0])
+        nc.scalar.copy(out=s_upper[1][:, 0, P:], in_=acc[:, P:])
+        add_h(acc, 1, 0, 1, 0)
+        store_done(1, 1, 0)
 
-        below = o_sb[0, 0, 1][:].rearrange("p c (m u r) -> p u c m r", u=4, r=4)
-        for t, part in mirror_parts(mirror_turn(s_upper)):
-            nc.vector.tensor_tensor(
-                out=below[:, t, t:],
-                in0=part.rearrange("p c (m r) -> p c m r", r=4),
-                in1=h_sb[0, 0][:, t + 1 :, t * P : (t + 1) * P].rearrange("p c (m r) -> p c m r", r=4),
-                op=ADD,
-            )
-        store_rows(0, 0, 1, 4)
-
-        flipped = [bank() for s in range(PACK)]
-        for t in range(PACK):
-            for s in range(PACK):
-                nc.tensor.transpose(flipped[s][:, t * P : (t + 1) * P], o_rows(0, 1, t)[:, s * P : (s + 1) * P], ident[:])
         lower = out[HALF:, :HALF].rearrange("(s p) n -> p s n", p=P)
         for s in range(PACK):
-            nc.scalar.copy(
+            acc = turn([o_rows(0, 1, t)[:, s * P : (s + 1) * P] for t in range(PACK)])
+            copy = nc.scalar.copy if s in (0, 2) else nc.vector.tensor_copy
+            copy(
                 out=o_rows(1, 0, s).rearrange("p (m t r) -> p m t r", t=4, r=4),
-                in_=flipped[s][:].rearrange("p (t m r) -> p m t r", t=4, r=4),
+                in_=acc[:].rearrange("p (t m r) -> p m t r", t=4, r=4),
             )
-        nc.sync.dma_start(out=lower[:, 0:2, :], in_=o_sb[1, 0, 0][:])
-        for t in range(PACK):
-            add_h(bracket_rows(1, t, 1, DIAG_COLS[0]), 1, t, 1, 0)
-            if t == 0:
-                store_rows(1, 1, 0, 1)
-                nc.sync.dma_start(out=lower[:, 2:4, :], in_=o_sb[1, 0, 2][:])
-            if t == 2:
-                store_rows(1, 1, 1, 3)
-        store_rows(1, 1, 3, 4)
+            for s0, s1 in STORE_CUTS[1, 0]:
+                if s1 == s + 1:
+                    nc.sync.dma_start(out=lower[:, s0:s1, :], in_=o_sb[1, 0, s0][:])
+        acc = turn([s_upper[1][:, 0, u * P : (u + 1) * P] for u in range(1, PACK)])
+        part = acc[:, : 3 * P].rearrange("p (u c) -> p u c", c=P)
+        for t0, t1 in STORE_CUTS[1, 1][1:]:
+            nc.vector.tensor_tensor(
+                out=o_sb[1, 1, t0][:].rearrange("p c (m u r) -> p u c m r", u=4, r=4)[:, 0],
+                in0=part[:, t0 - 1 : t1 - 1, :].rearrange("p c (m r) -> p c m r", r=4),
+                in1=h_sb[1, 1][:, 0, t0:t1, :].rearrange("p c (m r) -> p c m r", r=4),
+                op=ADD,
+            )
+        for t in range(1, PACK):
+            add_h(bracket_rows(1, t, 1, DIAG_COLS[1]), 1, t, 1, 1)
+            store_done(1, 1, t)

@@ -22,9 +22,9 @@ PACK = 4
 K_PASSES = K // HALF
 STORE_CUTS = {
     (0, 0): ((0, 1), (1, 4)),
-    (0, 1): ((0, 2), (2, 4)),
-    (1, 0): ((0, 2), (2, 4)),
-    (1, 1): ((0, 1), (1, 3), (3, 4)),
+    (0, 1): ((0, 1), (1, 2), (2, 3), (3, 4)),
+    (1, 0): ((0, 1), (1, 2), (2, 3), (3, 4)),
+    (1, 1): ((0, 1), (1, 2), (2, 3), (3, 4)),
 }
 DIAG_COLS = (((0, 512),), ((128, 256), (384, 128)), ((256, 256),), ((384, 128),))
 H_GROUPS = (
@@ -114,8 +114,8 @@ def tile_isospectral_bracket_step_s4_kernel(tc, a_words, a_scales, b_words, b_sc
             )
 
         def load_w(g, r):
-            rows = w[g * HALF : (g + 1) * HALF, :].rearrange("(m t r) n -> r m t n", t=4, r=4)
-            nc.sync.dma_start(out=w_raw[g][r:P:4, :, :], in_=rows[r])
+            rows = w[g * HALF : (g + 1) * HALF, :].rearrange("(m t r) n -> t m r n", t=4, r=4)
+            nc.sync.dma_start(out=w_raw[g][:, r, :], in_=rows[r])
 
         def load_d(r):
             runs = d.rearrange("(g m x) -> m g x", g=2, x=16)
@@ -298,9 +298,9 @@ def tile_isospectral_bracket_step_s4_kernel(tc, a_words, a_scales, b_words, b_sc
             )
 
         def store_rows(i, h, t0, t1):
-            rows = out[i * HALF : (i + 1) * HALF, h * HALF : (h + 1) * HALF].rearrange("(m t r) n -> r m t n", t=4, r=4)
-            for r in range(4):
-                nc.sync.dma_start(out=rows[r][:, t0:t1, :], in_=o_sb[i, h, t0][r:P:4, :, :])
+            rows = out[i * HALF : (i + 1) * HALF, h * HALF : (h + 1) * HALF].rearrange("(m t r) n -> t m r n", t=4, r=4)
+            for t in range(t0, t1):
+                nc.sync.dma_start(out=rows[t], in_=o_rows(i, h, t))
 
         def store_done(i, h, t):
             for t0, t1 in STORE_CUTS[i, h]:
@@ -343,10 +343,10 @@ def tile_isospectral_bracket_step_s4_kernel(tc, a_words, a_scales, b_words, b_sc
         for g, h in ((0, 0), (0, 1), (1, 0), (1, 1), (2, 0), (3, 0), (2, 1), (3, 1)):
             for x in range(2):
                 reorder(x, g, h)
-        nc.vector.tensor_copy(out=d_cols[:], in_=d_runs[:, :, 0:13:4])
         for h in range(2):
             for u in range(PACK):
                 pack_w(nc.vector.tensor_copy, 0, h, u)
+        nc.vector.tensor_copy(out=d_cols[:], in_=d_runs[:, :, 0:13:4])
         quantize_w(0, 0)
 
         upper = [bank() for t in range(PACK)]
@@ -438,13 +438,13 @@ def tile_isospectral_bracket_step_s4_kernel(tc, a_words, a_scales, b_words, b_sc
                 bracket_pass(pair[t], 0, t, 1, 0, HALF, j)
         for t, part in mirror_parts(mirror_turn(s_upper[0])):
             add_mirrored(0, t, part, o_sb[0, 0, 1][:, t:, :])
-        store_rows(0, 0, 1, 4)
+            store_rows(0, 0, t + 1, t + 2)
         for t in range(2):
             bracket_pass(pair[t], 0, t, 1, 0, HALF, 1)
         for t in range(2):
             bracket_pass(pair[t], 0, t, 1, 0, HALF, 3)
             add_h(pair[t], 0, t, 1, 0)
-        store_done(0, 1, 1)
+            store_done(0, 1, t)
         for t in range(2, PACK):
             add_h(bracket_rows(0, t, 1, DIAG_COLS[0]), 0, t, 1, 0)
             store_done(0, 1, t)

from contextlib import ExitStack

import concourse.mybir as mybir
from concourse.masks import make_identity

K, N = 2048, 1024
FLOPS = 2 * K * N * N + 2 * N * N * N

F32 = mybir.dt.float32
BF16 = mybir.dt.bfloat16
I32 = mybir.dt.int32
U32 = mybir.dt.uint32
U8 = mybir.dt.uint8
FP4X4 = mybir.dt.float4_e2m1fn_x4
FP8X4 = mybir.dt.float8_e4m3fn_x4
ADD = mybir.AluOpType.add
MULT = mybir.AluOpType.mult

P = 128
HALF = 512
PACK = 4
K_PASSES = K // HALF
STORE_CUTS = {
    (0, 0): ((0, 1), (1, 4)),
    (0, 1): ((0, 1), (1, 2), (2, 3), (3, 4)),
    (1, 0): ((0, 1), (1, 2), (2, 3), (3, 4)),
    (1, 1): ((0, 1), (1, 2), (2, 3), (3, 4)),
}
DIAG_COLS = (((0, 512),), ((128, 256), (384, 128)), ((256, 256),), ((384, 128),))
H_GROUPS = (
    (((0, 512), ((128, 128), (256, 256))),),
    (((256, 256), ((256, 256),)), ((128, 128), ())),
    (((256, 256), ((384, 128),)),),
    (((384, 128), ()),),
)
ROW_GROUPS = ((0,), (1,), (2, 3))
MIRROR = (((0, 1), (0, 2), (0, 3)), ((1, 2), (1, 3), (2, 3)))
WARM_PASSES = 18


def tile_isospectral_bracket_step_s4_kernel(tc, a_words, a_scales, b_words, b_scales, d, w, out):
    nc = tc.nc
    words = (a_words, b_words)
    scales = (a_scales, b_scales)

    with ExitStack() as ctx:
        keep = ctx.enter_context(tc.tile_pool(name="keep", bufs=1))
        psum = ctx.enter_context(tc.psum_pool(name="psum", bufs=8))
        ctx.enter_context(tc.manual_schedule())

        def sb(name, shape, dtype):
            return keep.tile(shape, dtype, name=name, align_bytes=64)

        def bank():
            return psum.tile([P, HALF], F32, name="bank")

        code_loads = {
            (x, g0): sb("raw_codes%d%d" % (x, g0), [P, g1 - g0, 2 * N], U8)
            for x in range(2)
            for g0, g1 in ((0, 1), (1, 2), (2, 4))
        }
        first_scales = [sb("first_scales%d" % x, [P, N], U8) for x in range(2)]
        later_scales = [sb("later_scales%d" % x, [P, K_PASSES - 1, N], U8) for x in range(2)]

        def raw_codes(x, g):
            return code_loads[x, min(g, 2)][:, g - min(g, 2), :]

        def raw_scales(x, g):
            return first_scales[x][:] if g == 0 else later_scales[x][:, g - 1, :]

        codes = [[sb("codes%d%d" % (x, h), [P, K_PASSES, 2 * HALF], U8) for h in range(2)] for x in range(2)]
        planes = [[sb("planes%d%d" % (x, h), [P, K_PASSES, HALF], U8) for h in range(2)] for x in range(2)]
        w_raw = [sb("w_raw%d" % g, [P, PACK, N], BF16) for g in range(2)]
        w_packed = [[sb("w_packed%d%d" % (g, h), [P, HALF, PACK], BF16) for h in range(2)] for g in range(2)]
        w_codes = [[sb("w_codes%d%d" % (g, h), [P, HALF], U32) for h in range(2)] for g in range(2)]
        w_planes = [[sb("w_planes%d%d" % (g, h), [P, HALF], U8) for h in range(2)] for g in range(2)]
        hd_packed = [[sb("hd_packed%d%d" % (g, h), [P, HALF, PACK], BF16) for h in range(2)] for g in range(2)]
        hd_codes = [[sb("hd_codes%d%d" % (g, h), [P, HALF], U32) for h in range(2)] for g in range(2)]
        hd_planes = [[sb("hd_planes%d%d" % (g, h), [P, HALF], U8) for h in range(2)] for g in range(2)]
        h_sb = {gh: sb("h_sb%d%d" % gh, [P, PACK, PACK, P], F32) for gh in ((0, 0), (0, 1), (1, 1))}
        o_sb = {
            (i, h, t0): sb("o_sb%d%d%d" % (i, h, t0), [P, t1 - t0, HALF], F32)
            for (i, h), cuts in STORE_CUTS.items()
            for t0, t1 in cuts
        }

        def o_rows(i, h, t):
            t0 = max(c0 for c0, c1 in STORE_CUTS[i, h] if c0 <= t)
            return o_sb[i, h, t0][:, t - t0, :]

        hd_rows = [sb("hd_rows%d" % g, [P, PACK, HALF // (g + 1)], BF16) for g in range(2)]
        d_runs = sb("d_runs", [P, 2, 16], BF16)
        d_cols = sb("d_cols", [P, 2, PACK], F32)
        s_upper = [sb("s_upper%d" % h, [P, PACK - 1 - 2 * h, HALF], F32) for h in range(2)]
        warm_in = sb("warm_in", [P, PACK * P], BF16)
        warm_codes = sb("warm_codes", [P, P], U32)
        warm_plane = sb("warm_plane", [P, P], U8)
        ident = sb("ident", [P, P], F32)

        def load_words(x, g0, g1):
            nc.sync.dma_start(
                out=code_loads[x, g0][:].bitcast(I32),
                in_=words[x][g0:g1].bitcast(I32).rearrange("g p n -> p g n"),
            )

        def load_first_scales(queue, x, q):
            rows = scales[x].bitcast(I32).rearrange("g q n -> (g q) n")
            queue.dma_start(out=first_scales[x][32 * q : 32 * (q + 1), :].bitcast(I32), in_=rows[4 * q : 4 * q + 32, :])

        def load_later_scales(queue, x, r):
            queue.dma_start(
                out=later_scales[x][r:P:32, :, :].bitcast(I32),
                in_=scales[x].bitcast(I32).rearrange("g (q r) n -> r q g n", r=4)[r][:, 1:, :],
            )

        def load_w(g, r):
            rows = w[g * HALF : (g + 1) * HALF, :].rearrange("(m t r) n -> t m r n", t=4, r=4)
            nc.sync.dma_start(out=w_raw[g][:, r, :], in_=rows[r])

        def load_d(r):
            runs = d.rearrange("(g m x) -> m g x", g=2, x=16)
            nc.sync.dma_start(out=d_runs[r:P:4, :, 0:13], in_=runs[:, :, r : r + 13])

        def reorder(x, g, h):
            nc.vector.tensor_copy(
                out=planes[x][h][:, g, :].bitcast(I32).rearrange("p (t m) -> p t m", t=4),
                in_=raw_scales(x, g)[:, h * HALF : (h + 1) * HALF].bitcast(I32).rearrange("p (m t) -> p t m", t=4),
            )
            nc.vector.tensor_copy(
                out=codes[x][h][:, g, :].bitcast(I32).rearrange("p (t m e) -> p t m e", t=4, e=2),
                in_=raw_codes(x, g)[:, h * N : (h + 1) * N].bitcast(I32).rearrange("p (m t e) -> p t m e", t=4, e=2),
            )

        def ordered(x, g, h, c0, n):
            return codes[x][h][:, g, 2 * c0 : 2 * (c0 + n)].bitcast(FP4X4), planes[x][h][:, g, c0 : c0 + n]

        def natural(x, g, h):
            return (
                raw_codes(x, g)[:, h * N : (h + 1) * N].bitcast(FP4X4),
                raw_scales(x, g)[:, h * HALF : (h + 1) * HALF],
            )

        def mx(acc, stationary, moving, start, stop):
            nc.tensor.matmul_mx(
                out=acc,
                lhsT=stationary[0],
                lhsT_scale=stationary[1],
                rhs=moving[0],
                rhs_scale=moving[1],
                start=start,
                stop=stop,
            )

        def off_diag_pass(acc, t, g, x):
            mx(acc[:], ordered(x, g, 0, t * P, P), natural(1 - x, g, 1), g == 0 and x == 0, g == K_PASSES - 1 and x == 1)

        def diag_passes(acc, h, t, group, g):
            ab, ba = group
            passes = [(0, ab)] + [(1, cols) for cols in ba]
            for x, (c0, n) in passes[::-1] if g == K_PASSES - 1 else passes:
                mx(
                    acc[:, c0 : c0 + n],
                    ordered(x, g, h, t * P, P),
                    ordered(1 - x, g, h, c0, n),
                    g == 0 and x == 0,
                    g == K_PASSES - 1 and x == 0,
                )

        def diag_rows(h, t):
            acc = bank()
            for group in H_GROUPS[t]:
                for g in range(K_PASSES):
                    diag_passes(acc, h, t, group, g)
            return acc

        def keep_diag(acc, h, t):
            nc.scalar.copy(out=h_sb[h, h][:, t:, t, :], in_=acc[:, t * P :].rearrange("p (u c) -> p u c", c=P))

        def keep_off_diag(acc, t):
            nc.scalar.copy(
                out=h_sb[0, 1][:, :, t, :].rearrange("p u (m r) -> p u m r", r=4),
                in_=acc[:].rearrange("p (m u r) -> p u m r", u=4, r=4),
            )

        def scale_off_diag(acc, t):
            nc.scalar.activation(
                out=hd_rows[0][:, t, :].rearrange("p (u m r) -> p u m r", u=4, r=4),
                in_=acc[:].rearrange("p (m u r) -> p u m r", u=4, r=4),
                func=mybir.ActivationFunctionType.Copy,
                scale=d_cols[:, 0, t : t + 1],
            )

        def scale_last_cols(t):
            nc.scalar.activation(
                out=hd_rows[1][:, t, :].rearrange("p (u c) -> p u c", c=P),
                in_=h_sb[1, 1][:, 2:, t, :],
                func=mybir.ActivationFunctionType.Copy,
                scale=d_cols[:, 1, t : t + 1],
            )

        def pack_hd_rows(g, c0):
            nc.vector.tensor_copy(
                out=hd_packed[g][1][:, c0:, :].rearrange("p (c e) t -> p c t e", e=4),
                in_=hd_rows[g][:].rearrange("p t (c e) -> p c t e", e=4),
            )

        def turn(blocks):
            acc = bank()
            for i, block in enumerate(blocks):
                nc.tensor.transpose(acc[:, i * P : (i + 1) * P], block, ident[:])
            return acc

        def mirror_turn(src):
            return [turn([src[:, t, u * P : (u + 1) * P] for t, u in pairs]) for pairs in MIRROR]

        def mirror_parts(accs):
            return [
                (t, acc[:, c0 * P : (c0 + PACK - 1 - t) * P].rearrange("p (u c) -> p u c", c=P))
                for t, acc, c0 in ((0, accs[0], 0), (1, accs[1], 0), (2, accs[1], 2))
            ]

        def turn_rows(h, rows):
            return turn([h_sb[h, h][:, u, t, :] for t in rows for u in range(t, PACK)])

        def complete_rows(acc, h, rows):
            starts = [sum(PACK - t for t in rows[:i]) * P for i in range(len(rows))]
            t = rows[0]
            nc.scalar.copy(
                out=h_sb[h, h][:, t, t + 1 :, :],
                in_=acc[:, P : (PACK - t) * P].rearrange("p (u c) -> p u c", c=P),
            )
            for t, c0 in zip(rows, starts):
                block = h_sb[h, h][:, t, t, :]
                nc.vector.tensor_tensor(out=block, in0=acc[:, c0 : c0 + P], in1=block, op=ADD)

        def pack_hd(g, h, u):
            nc.vector.tensor_tensor(
                out=hd_packed[g][h][:, u * P : (u + 1) * P, :].rearrange("p (c e) t -> p c t e", e=2),
                in0=h_sb[g, h][:, u].rearrange("p t (c e) -> p c t e", e=2),
                in1=d_cols[:, g, :].unsqueeze(1).unsqueeze(3).to_broadcast([P, P // 2, PACK, 2]),
                op=MULT,
            )

        def pack_hd_turned(acc, t):
            nc.vector.tensor_tensor(
                out=hd_packed[1][0][:, t * P : (t + 1) * P, :],
                in0=acc[:].rearrange("p (u c) -> p c u", u=4),
                in1=d_cols[:, 1, :].unsqueeze(1).to_broadcast([P, P, PACK]),
                op=MULT,
            )

        def pack_w(copy, g, h, u):
            cols = w_raw[g][:, :, h * HALF : (h + 1) * HALF].rearrange("p t (m u r) -> p u m t r", u=4, r=4)
            copy(
                out=w_packed[g][h][:, u * P : (u + 1) * P, :].rearrange("p (m r) t -> p m t r", r=4),
                in_=cols[:, u],
            )

        def quantize(dst_codes, dst_plane, src):
            nc.vector.quantize_mx(
                out=dst_codes[:].bitcast(FP8X4),
                scales=dst_plane[:],
                in_=src[:].rearrange("p c t -> p (c t)"),
            )

        def quantize_w(g, h):
            quantize(w_codes[g][h], w_planes[g][h], w_packed[g][h])

        def quantize_hd(g, h):
            quantize(hd_codes[g][h], hd_planes[g][h], hd_packed[g][h])

        def bracket_pass(acc, i, t, h, c0, n, j):
            g = j % 2
            sides = ((hd_codes, hd_planes), (w_codes, w_planes))
            (s_codes, s_planes), (m_codes, m_planes) = sides[j // 2], sides[1 - j // 2]
            rows, cols = slice(t * P, (t + 1) * P), slice(c0, c0 + n)
            mx(
                acc[:, cols],
                (s_codes[g][i][:, rows].bitcast(FP8X4), s_planes[g][i][:, rows]),
                (m_codes[g][h][:, cols].bitcast(FP8X4), m_planes[g][h][:, cols]),
                j == 0,
                j == 3,
            )

        def bracket_rows(i, t, h, ranges):
            acc = bank()
            for c0, n in ranges:
                for j in range(4):
                    bracket_pass(acc, i, t, h, c0, n, j)
            return acc

        def add_h(acc, i, t, h, u0):
            nc.vector.tensor_tensor(
                out=o_rows(i, h, t).rearrange("p (m u r) -> p m u r", u=4, r=4)[:, :, u0:, :],
                in0=acc[:].rearrange("p (u m r) -> p m u r", u=4, r=4)[:, :, u0:, :],
                in1=h_sb[i, h][:, u0:, t, :].rearrange("p u (m r) -> p m u r", r=4),
                op=ADD,
            )

        def store_rows(i, h, t0, t1):
            rows = out[i * HALF : (i + 1) * HALF, h * HALF : (h + 1) * HALF].rearrange("(m t r) n -> t m r n", t=4, r=4)
            for t in range(t0, t1):
                nc.sync.dma_start(out=rows[t], in_=o_rows(i, h, t))

        def store_done(i, h, t):
            for t0, t1 in STORE_CUTS[i, h]:
                if t1 == t + 1:
                    store_rows(i, h, t0, t1)

        for q in range(2):
            load_first_scales(nc.sync, 0, q)
        load_words(0, 0, 1)
        for q in range(2, 4):
            load_first_scales(nc.sync, 0, q)
        load_words(1, 0, 1)
        for q in range(4):
            load_first_scales(nc.sync, 1, q)
        nc.vector.memset(warm_in[:], 1.0)
        nc.vector.quantize_mx(out=warm_codes[:].bitcast(FP8X4), scales=warm_plane[:], in_=warm_in[:])
        nc.vector.memset(later_scales[1][:].bitcast(I32), 0)
        nc.vector.memset(later_scales[0][:].bitcast(I32), 0)
        for x in range(2):
            load_words(x, 1, 2)
        for r in range(4):
            load_later_scales(nc.sync, 0, r)
        for r in range(4):
            load_later_scales(nc.sync if r < 2 else nc.gpsimd, 1, r)
        for x in range(2):
            load_words(x, 2, K_PASSES)
        for r in range(4):
            load_w(0, r)
        for r in range(4):
            load_d(r)
        for r in range(4):
            load_w(1, r)
        make_identity(nc, ident[:])

        acc = bank()
        warm = (warm_codes[:].bitcast(FP8X4), warm_plane[:])
        for i in range(WARM_PASSES):
            mx(acc[:, :P], warm, warm, True, True)

        for g, h in ((0, 0), (0, 1), (1, 0), (1, 1), (2, 0), (3, 0), (2, 1), (3, 1)):
            for x in range(2):
                reorder(x, g, h)
        for h in range(2):
            for u in range(PACK):
                pack_w(nc.vector.tensor_copy, 0, h, u)
        nc.vector.tensor_copy(out=d_cols[:], in_=d_runs[:, :, 0:13:4])
        quantize_w(0, 0)

        upper = [bank() for t in range(PACK)]
        diag = [bank() for t in range(PACK)]
        for g in range(2):
            for x in range(2):
                for t in range(PACK):
                    off_diag_pass(upper[t], t, g, x)
            for t in range(PACK):
                diag_passes(diag[t], 0, t, H_GROUPS[t][0], g)
        for t in range(PACK):
            for i, group in enumerate(H_GROUPS[t]):
                for g in range(2 if i == 0 else 0, K_PASSES):
                    diag_passes(diag[t], 0, t, group, g)
            keep_diag(diag[t], 0, t)
        for g in range(2, K_PASSES):
            for x in range(2):
                off_diag_pass(upper[0], 0, g, x)
        keep_off_diag(upper[0], 0)
        turned = [turn_rows(0, rows) for rows in ROW_GROUPS]
        for acc, rows in zip(turned, ROW_GROUPS):
            complete_rows(acc, 0, rows)
        scale_off_diag(upper[0], 0)
        for u in range(PACK):
            pack_hd(0, 0, u)
        quantize_w(0, 1)
        quantize_hd(0, 0)
        for t in range(1, PACK):
            for g in range(2, K_PASSES):
                for x in range(2):
                    off_diag_pass(upper[t], t, g, x)
            keep_off_diag(upper[t], t)
            if t < PACK - 1:
                scale_off_diag(upper[t], t)

        acc = diag_rows(1, 0)
        scale_off_diag(upper[PACK - 1], PACK - 1)
        pack_w(nc.scalar.copy, 1, 0, 0)
        keep_diag(acc, 1, 0)
        pack_hd_rows(0, 0)
        turned = [turn([h_sb[0, 1][:, u, t, :] for u in range(PACK)]) for t in range(PACK)]
        acc = turn_rows(1, ROW_GROUPS[0])
        for t in range(PACK):
            pack_hd_turned(turned[t], t)
        for u in range(1, 3):
            pack_w(nc.scalar.copy, 1, 0, u)
        complete_rows(acc, 1, ROW_GROUPS[0])
        pack_w(nc.scalar.copy, 1, 0, 3)
        quantize_hd(0, 1)
        quantize_hd(1, 0)
        quantize_w(1, 0)
        pack_w(nc.scalar.copy, 1, 1, 0)
        pack_w(nc.vector.tensor_copy, 1, 1, 1)
        pack_hd(1, 1, 0)
        for t in range(1, PACK):
            keep_diag(diag_rows(1, t), 1, t)
        turned = [turn_rows(1, rows) for rows in ROW_GROUPS[1:]]
        for acc, rows in zip(turned, ROW_GROUPS[1:]):
            complete_rows(acc, 1, rows)
        pack_hd(1, 1, 1)

        def add_mirrored(i, t, part, dst):
            nc.vector.tensor_tensor(
                out=dst.rearrange("p c (m u r) -> p u c m r", u=4, r=4)[:, t],
                in0=part.rearrange("p c (m r) -> p c m r", r=4),
                in1=h_sb[i, i][:, t, t + 1 :, :].rearrange("p c (m r) -> p c m r", r=4),
                op=ADD,
            )

        accs = []
        for t in range(PACK):
            accs.append(bracket_rows(0, t, 0, DIAG_COLS[t]))
            if t < PACK - 1:
                if t < 2:
                    pack_w(nc.scalar.copy, 1, 1, t + 2)
                nc.scalar.copy(out=s_upper[0][:, t, (t + 1) * P :], in_=accs[t][:, (t + 1) * P :])
        pack_hd(1, 1, 2)
        pack_hd(1, 1, 3)
        add_h(accs[0], 0, 0, 0, 0)
        store_rows(0, 0, 0, 1)
        quantize_w(1, 1)
        quantize_hd(1, 1)
        add_h(accs[1], 0, 1, 0, 1)
        add_h(accs[2], 0, 2, 0, 2)
        add_h(accs[3], 0, 3, 0, 3)
        pair = [bank() for t in range(2)]
        for t in range(2):
            for j in (0, 2):
                bracket_pass(pair[t], 0, t, 1, 0, HALF, j)
        for t, part in mirror_parts(mirror_turn(s_upper[0])):
            add_mirrored(0, t, part, o_sb[0, 0, 1][:, t:, :])
            store_rows(0, 0, t + 1, t + 2)
        for t in range(2):
            bracket_pass(pair[t], 0, t, 1, 0, HALF, 1)
        for t in range(2):
            bracket_pass(pair[t], 0, t, 1, 0, HALF, 3)
            add_h(pair[t], 0, t, 1, 0)
            store_done(0, 1, t)
        for t in range(2, PACK):
            add_h(bracket_rows(0, t, 1, DIAG_COLS[0]), 0, t, 1, 0)
            store_done(0, 1, t)
        acc = bracket_rows(1, 0, 1, DIAG_COLS[0])
        nc.scalar.copy(out=s_upper[1][:, 0, P:], in_=acc[:, P:])
        add_h(acc, 1, 0, 1, 0)
        store_done(1, 1, 0)

        lower = out[HALF:, :HALF].rearrange("(s p) n -> p s n", p=P)
        for s in range(PACK):
            acc = turn([o_rows(0, 1, t)[:, s * P : (s + 1) * P] for t in range(PACK)])
            copy = nc.scalar.copy if s in (0, 2) else nc.vector.tensor_copy
            copy(
                out=o_rows(1, 0, s).rearrange("p (m t r) -> p m t r", t=4, r=4),
                in_=acc[:].rearrange("p (t m r) -> p m t r", t=4, r=4),
            )
            for s0, s1 in STORE_CUTS[1, 0]:
                if s1 == s + 1:
                    nc.sync.dma_start(out=lower[:, s0:s1, :], in_=o_sb[1, 0, s0][:])
        acc = turn([s_upper[1][:, 0, u * P : (u + 1) * P] for u in range(1, PACK)])
        part = acc[:, : 3 * P].rearrange("p (u c) -> p u c", c=P)
        for t0, t1 in STORE_CUTS[1, 1][1:]:
            nc.vector.tensor_tensor(
                out=o_sb[1, 1, t0][:].rearrange("p c (m u r) -> p u c m r", u=4, r=4)[:, 0],
                in0=part[:, t0 - 1 : t1 - 1, :].rearrange("p c (m r) -> p c m r", r=4),
                in1=h_sb[1, 1][:, 0, t0:t1, :].rearrange("p c (m r) -> p c m r", r=4),
                op=ADD,
            )
        for t in range(1, PACK):
            add_h(bracket_rows(1, t, 1, DIAG_COLS[1]), 1, t, 1, 1)
            store_done(1, 1, t)
